import numpy as np
import ml_dtypes


def mxq(x, axis, fmt="e4m3"):
    dtype, down = {"e4m3": (ml_dtypes.float8_e4m3fn, 7), "e5m2": (ml_dtypes.float8_e5m2, 14)}[fmt]
    v = np.moveaxis(np.asarray(x, np.float32).astype(ml_dtypes.bfloat16).astype(np.float64), axis, -1)
    blocks = v.reshape(v.shape[:-1] + (-1, 32))
    amax = np.abs(blocks).max(-1, keepdims=True)
    byte = np.maximum(np.where(amax > 0, np.frexp(amax)[1] - 1 + 127, 0) - down, 1)
    scale = np.exp2(byte - 127.0)
    codes = (blocks / scale).astype(np.float32).astype(dtype).astype(np.float64)
    return np.moveaxis((codes * scale).reshape(v.shape), -1, axis)


WIDE = False


def mx_kscale(k):
    if not WIDE:
        return np.ones(k)
    levels = np.array([10, -10, 5, -5, 0])
    if k % 512:
        return np.exp2(np.random.permutation(np.resize(levels, k // 32))).repeat(32)
    a = np.empty((k // 512, 16))
    for p in range(k // 512):
        a[p, :8] = np.random.permutation(np.resize(levels, 8))
        for g in range(8):
            far = levels[np.abs(levels - a[p, g]) >= 10]
            a[p, g + 8] = far[np.random.randint(len(far))]
    return np.exp2(a.ravel()).repeat(32)


def f64(x):
    return np.asarray(x).astype(np.float64)


def striped8(idx):
    return np.asarray(idx).reshape(8, -1, 16).transpose(0, 2, 1).reshape(128, -1).astype(np.uint16)


def unstriped8(offs):
    return offs.reshape(8, 16, -1).transpose(0, 2, 1).reshape(8, -1).astype(np.int64)


def pick8(x, idx, run):
    r = np.arange(len(x))
    return x[r[:, None], idx[r % (8 * run) // run]]


E2M1 = np.array([0.0, 0.5, 1.0, 1.5, 2.0, 3.0, 4.0, 6.0, -0.0, -0.5, -1.0, -1.5, -2.0, -3.0, -4.0, -6.0])


def pack_weight(w, fmt):
    k, n = w.shape
    w = f64(np.asarray(w, np.float32).astype(ml_dtypes.bfloat16)).reshape(k // 32, 32, n)
    amax = np.abs(w).max(1)
    if fmt == "e4m3":
        byte = np.frexp(amax)[1] - 1 + 127 - 7
    else:
        mant, ex = np.frexp(amax / 6.0)
        byte = np.where(mant > 0.5, ex, ex - 1) + 127
    byte = np.clip(np.where(amax > 0, byte, 1), 1, 254)
    scaled = (w * np.exp2(127.0 - byte)[:, None, :]).reshape(k, n).astype(np.float32)
    by_word = np.ascontiguousarray(scaled.reshape(k // 512, 128, 4, n).transpose(0, 1, 3, 2))
    if fmt == "e4m3":
        words = by_word.astype(ml_dtypes.float8_e4m3fn).view(np.uint8)
    else:
        c = by_word.astype(ml_dtypes.float4_e2m1fn).view(np.uint8) & 0xF
        words = (c[..., 0::2] | (c[..., 1::2] << 4)).reshape(k // 512, 128, 2 * n)
    return np.ascontiguousarray(words), np.ascontiguousarray(byte.astype(np.uint8).reshape(k // 512, 16, n))


def unpack_weight(words, scales, fmt):
    g, _, n = scales.shape
    words = np.ascontiguousarray(words).reshape(g, 128, n, -1)
    if fmt == "e4m3":
        vals = words.view(ml_dtypes.float8_e4m3fn).astype(np.float64)
    else:
        nib = np.empty((g, 128, n, 4), np.uint8)
        nib[..., 0::2] = words & 0xF
        nib[..., 1::2] = words >> 4
        vals = E2M1[nib]
    vals = vals * np.repeat(np.exp2(scales.astype(np.float64) - 127.0), 8, axis=1)[..., None]
    return vals.transpose(0, 1, 3, 2).reshape(g * 512, n)


def sigmoid(v):
    return 1.0 / (1.0 + np.exp(-v))


def bf(x):
    return np.asarray(x, np.float32).astype(ml_dtypes.bfloat16)


def planes(Y):
    r, m = Y.shape
    b = f64(bf(Y)).reshape(r // 32, 32, m)
    amax = np.abs(b).max(1)
    byte = np.clip(np.where(amax > 0, np.frexp(amax)[1] - 1 + 127 - 7, 1), 1, 254)
    codes = (b * np.exp2(127.0 - byte)[:, None, :]).reshape(r, m).astype(np.float32).astype(ml_dtypes.float8_e4m3fn).view(np.uint8)
    words = codes.reshape(r // 512, 128, 4, m).transpose(0, 1, 3, 2)
    return np.ascontiguousarray(words), np.ascontiguousarray(byte.astype(np.uint8).reshape(r // 512, 16, m))


K, T, J, L, N = 512, 1024, 512, 512, 512


def setup_inputs():
    n = np.random.standard_normal
    idx = np.stack([np.random.permutation(T)[:J] for _ in range(8)])
    fk = mx_kscale(K)
    fl = mx_kscale(L)
    wp = pack_weight(n((K, N)) * 1 / np.sqrt(K) * fk[:, None], "e2m1")
    sxp = pack_weight(n((L, J)) / fl[:, None], "e4m3")
    wsp = pack_weight(n((L, N)) * 1 / np.sqrt(L) * fl[:, None], "e2m1")
    return {
        "xt": (n((K, T)) / fk[:, None]).astype(np.float32),
        "w_words": wp[0],
        "w_scales": wp[1],
        "sx_words": sxp[0],
        "sx_scales": sxp[1],
        "ws_words": wsp[0],
        "ws_scales": wsp[1],
        "offs": striped8(idx),
    }


def reference(xt, w_words, w_scales, sx_words, sx_scales, ws_words, ws_scales, offs):
    idx = unstriped8(offs)
    wu = unpack_weight(w_words, w_scales, "e2m1")
    sxu = unpack_weight(sx_words, sx_scales, "e4m3")
    wsu = unpack_weight(ws_words, ws_scales, "e2m1")
    xtidxq = mxq(pick8(f64(xt), idx, 64), 0, "e4m3")
    p = wu.T @ xtidxq
    q = wsu.T @ sxu
    y = p * sigmoid(q)
    words, scales = planes(y)
    return y, words, scales

@@ -1,0 +1,181 @@
+from contextlib import ExitStack
+
+import concourse.mybir as mybir
+
+K, T, J, L, N = 512, 1024, 512, 512, 512
+FLOPS = 2 * K * N * J + 2 * L * N * J
+
+F32 = mybir.dt.float32
+BF16 = mybir.dt.bfloat16
+I32 = mybir.dt.int32
+U32 = mybir.dt.uint32
+U16 = mybir.dt.uint16
+U8 = mybir.dt.uint8
+FP8X4 = mybir.dt.float8_e4m3fn_x4
+FP4X4 = mybir.dt.float4_e2m1fn_x4
+SIGMOID = mybir.ActivationFunctionType.Sigmoid
+COPY = mybir.ActivationFunctionType.Copy
+MULT = mybir.AluOpType.mult
+
+P = 128
+PACK = 4
+HALF = 256
+CH = 128
+NCH = J // CH
+
+
+def tile_moe_expert_heads_gated_pl_kernel(tc, xt, w_words, w_scales, sx_words, sx_scales, ws_words, ws_scales, offs, out_0, out_1, out_2):
+    nc = tc.nc
+    with ExitStack() as ctx:
+        keep = ctx.enter_context(tc.tile_pool(name="keep", bufs=1))
+        psum = ctx.enter_context(tc.psum_pool(name="psum", bufs=1))
+
+        def sb(name, shape, dtype, tag=None):
+            return keep.tile(shape, dtype, name=name, tag=tag or name, align_bytes=64)
+
+        offsets = keep.tile([P, J // 16], U16, name="offsets")
+        w_raw = sb("w_raw", [P, 2 * N], U8)
+        ws_raw = sb("ws_raw", [P, 2 * N], U8)
+        w_sraw = sb("w_sraw", [P, N], U8)
+        ws_sraw = sb("ws_sraw", [P, N], U8)
+        sx_c = sb("sx_c", [P, J], U32)
+        sx_s = sb("sx_s", [P, J], U8)
+        x = [sb("x%d" % t, [P, T], F32) for t in range(PACK)]
+        warm = sb("warm", [P, 1], F32)
+        warm2 = sb("warm2", [P, 1], F32)
+
+        def load_scales(eng, tile, src):
+            for q in range(4):
+                eng.dma_start(out=tile[32 * q : 32 * q + 4, :].bitcast(I32), in_=src[0, 4 * q : 4 * q + 4, :].bitcast(I32))
+
+        xv = xt.rearrange("(p t) c -> p t c", t=PACK)
+        nc.vector.memset(warm[:], 0.0)
+        nc.vector.memset(ws_sraw[:].bitcast(I32), 0)
+        nc.vector.memset(sx_s[:].bitcast(I32), 0)
+        nc.gpsimd.memset(w_sraw[:].bitcast(I32), 0)
+        nc.scalar.activation(warm2[:], warm[:], SIGMOID)
+        nc.sync.dma_start(out=x[0][:], in_=xv[:, 0, :])
+        nc.sync.dma_start(out=ws_raw[:].bitcast(I32), in_=ws_words[0].bitcast(I32))
+        nc.sync.dma_start(offsets[:], offs)
+        load_scales(nc.sync, ws_sraw, ws_scales)
+        load_scales(nc.gpsimd, w_sraw, w_scales)
+        nc.sync.dma_start(out=x[1][:], in_=xv[:, 1, :])
+        nc.sync.dma_start(out=w_raw[:].bitcast(I32), in_=w_words[0].bitcast(I32))
+        nc.sync.dma_start(out=sx_c[:].bitcast(I32), in_=sx_words[0].rearrange("p c r -> p (c r)").bitcast(I32))
+        load_scales(nc.sync, sx_s, sx_scales)
+        for t in range(2, PACK):
+            nc.sync.dma_start(out=x[t][:], in_=xv[:, t, :])
+
+        def deal_words(name, raw):
+            dealt = sb(name, [P, 2 * N], U8)
+            nc.vector.tensor_copy(out=dealt[:].bitcast(U16).rearrange("p (t m) -> p t m", t=PACK), in_=raw[:].bitcast(U16).rearrange("p (m t) -> p t m", t=PACK))
+            return dealt
+
+        def deal_scales(name, raw, tag=None):
+            dealt = sb(name, [P, N], U8, tag)
+            nc.vector.tensor_copy(out=dealt[:].rearrange("p (t m) -> p t m", t=PACK), in_=raw[:].rearrange("p (m t) -> p t m", t=PACK))
+            return dealt
+
+        ws_c = deal_words("ws_c", ws_raw)
+        ws_s = deal_scales("ws_s", ws_sraw)
+
+        picked = [sb("picked%d" % h, [P, PACK, HALF], BF16) for h in range(2)]
+
+        def gather(t, h):
+            nc.vector.tensor_copy(picked[h][:, t, :], x[t][:].indirect(offsets[:, 16 * h : 16 * (h + 1)]))
+
+        x0_bf = sb("x0_bf", [P, T], BF16)
+        nc.scalar.activation(x0_bf[:], x[0][:], COPY)
+        for h in range(2):
+            nc.scalar.activation(picked[h][:, 0, :], x0_bf[:].indirect(offsets[:, 16 * h : 16 * (h + 1)]), COPY)
+
+        gate = sb("gate", [P, PACK, J], F32)
+        for t in range(PACK):
+            qb = psum.tile([P, J], F32, name="q%d" % t)
+            nc.tensor.matmul_mx(out=qb[:], lhsT=ws_c[:, 256 * t : 256 * (t + 1)].bitcast(FP4X4), lhsT_scale=ws_s[:, P * t : P * (t + 1)],
+                                rhs=sx_c[:].bitcast(FP8X4), rhs_scale=sx_s[:], start=True, stop=True)
+            nc.scalar.activation(gate[:, t, :], qb[:], SIGMOID)
+
+        gather(1, 0)
+        gather(1, 1)
+        w_c = deal_words("w_c", w_raw)
+        gather(2, 0)
+        gather(2, 1)
+        w_s = deal_scales("w_s", w_sraw, "x2")
+
+        xw = [sb("xw%d" % c, [P, CH, PACK], BF16) for c in range(NCH)]
+        xc = [sb("xc%d" % c, [P, CH], U32) for c in range(NCH)]
+        xs = [sb("xs%d" % c, [P, CH], U8) for c in range(NCH)]
+        y = [sb("y%d" % h, [P, PACK, HALF], F32) for h in range(2)]
+        yw = [sb("yw%d" % c, [P, CH, PACK], BF16) for c in range(NCH)]
+        y_c = sb("y_c", [P, J], U32)
+        y_s = sb("y_s", [P, J], U8)
+        ov = out_0.rearrange("(p t) j -> p t j", t=PACK)
+        o1 = out_1[0].rearrange("p c r -> p (c r)").bitcast(I32)
+        pb = {}
+
+        def cols(c):
+            return slice(CH * (c % 2), CH * (c % 2 + 1))
+
+        def weave(c, on_vector):
+            src = picked[c // 2][:, :, cols(c)].rearrange("p t j -> p j t")
+            if on_vector:
+                nc.vector.tensor_copy(out=xw[c][:], in_=src)
+            else:
+                nc.scalar.copy(out=xw[c][:], in_=src)
+
+        def quant(c):
+            nc.vector.quantize_mx(out=xc[c][:].bitcast(FP8X4), scales=xs[c][:], in_=xw[c][:].rearrange("p j t -> p (j t)"))
+            pb[c] = psum.tile([P, PACK, CH], F32, name="p%d" % c)
+            for t in range(PACK):
+                nc.tensor.matmul_mx(out=pb[c][:, t, :], lhsT=w_c[:, 256 * t : 256 * (t + 1)].bitcast(FP4X4), lhsT_scale=w_s[:, P * t : P * (t + 1)],
+                                    rhs=xc[c][:].bitcast(FP8X4), rhs_scale=xs[c][:], start=True, stop=True)
+
+        def gated(c):
+            nc.vector.tensor_tensor(y[c // 2][:, :, cols(c)], pb[c][:], gate[:, :, CH * c : CH * (c + 1)], MULT)
+
+        def store_y(h):
+            nc.sync.dma_start(out=ov[:, :, HALF * h : HALF * (h + 1)], in_=y[h][:])
+
+        def round_y(c, on_vector):
+            src = y[c // 2][:, :, cols(c)].rearrange("p t j -> p j t")
+            if on_vector:
+                nc.vector.tensor_copy(out=yw[c][:], in_=src)
+            else:
+                nc.scalar.copy(out=yw[c][:], in_=src)
+
+        def quant_y(c):
+            nc.vector.quantize_mx(out=y_c[:, CH * c : CH * (c + 1)].bitcast(FP8X4), scales=y_s[:, CH * c : CH * (c + 1)], in_=yw[c][:].rearrange("p j t -> p (j t)"))
+
+        def store_words(h):
+            nc.sync.dma_start(out=o1[:, HALF * h : HALF * (h + 1)], in_=y_c[:, HALF * h : HALF * (h + 1)].bitcast(I32))
+
+        gather(3, 0)
+        weave(0, True)
+        weave(1, False)
+        gather(3, 1)
+        quant(0)
+        weave(2, False)
+        weave(3, False)
+        quant(1)
+        gated(0)
+        quant(2)
+        gated(1)
+        store_y(0)
+        round_y(0, False)
+        quant(3)
+        gated(2)
+        round_y(1, False)
+        gated(3)
+        store_y(1)
+        round_y(2, False)
+        quant_y(0)
+        quant_y(1)
+        store_words(0)
+        round_y(3, True)
+        quant_y(2)
+        quant_y(3)
+        store_words(1)
+        for q in range(4):
+            eng = nc.scalar if q % 2 else nc.sync
+            eng.dma_start(out=out_2[0, 4 * q : 4 * q + 4, :].bitcast(I32), in_=y_s[32 * q : 32 * q + 4, :].bitcast(I32))

@@ -52,19 +52,19 @@ def tile_moe_expert_heads_gated_pl_kernel(tc, xt, w_words, w_scales, sx_words, s
         nc.vector.memset(warm[:], 0.0)
         nc.vector.memset(ws_sraw[:].bitcast(I32), 0)
         nc.vector.memset(sx_s[:].bitcast(I32), 0)
-        nc.gpsimd.memset(w_sraw[:].bitcast(I32), 0)
+        nc.vector.memset(w_sraw[:].bitcast(I32), 0)
         nc.scalar.activation(warm2[:], warm[:], SIGMOID)
-        nc.sync.dma_start(out=x[0][:], in_=xv[:, 0, :])
-        nc.sync.dma_start(out=ws_raw[:].bitcast(I32), in_=ws_words[0].bitcast(I32))
         nc.sync.dma_start(offsets[:], offs)
+        nc.sync.dma_start(out=ws_raw[:].bitcast(I32), in_=ws_words[0].bitcast(I32))
+        nc.sync.dma_start(out=x[0][:], in_=xv[:, 0, :])
         load_scales(nc.sync, ws_sraw, ws_scales)
-        load_scales(nc.gpsimd, w_sraw, w_scales)
         nc.sync.dma_start(out=x[1][:], in_=xv[:, 1, :])
         nc.sync.dma_start(out=w_raw[:].bitcast(I32), in_=w_words[0].bitcast(I32))
+        nc.sync.dma_start(out=x[2][:], in_=xv[:, 2, :])
         nc.sync.dma_start(out=sx_c[:].bitcast(I32), in_=sx_words[0].rearrange("p c r -> p (c r)").bitcast(I32))
         load_scales(nc.sync, sx_s, sx_scales)
-        for t in range(2, PACK):
-            nc.sync.dma_start(out=x[t][:], in_=xv[:, t, :])
+        nc.sync.dma_start(out=x[3][:], in_=xv[:, 3, :])
+        load_scales(nc.sync, w_sraw, w_scales)
 
         def deal_words(name, raw):
             dealt = sb(name, [P, 2 * N], U8)
@@ -89,93 +89,92 @@ def tile_moe_expert_heads_gated_pl_kernel(tc, xt, w_words, w_scales, sx_words, s
         for h in range(2):
             nc.scalar.activation(picked[h][:, 0, :], x0_bf[:].indirect(offsets[:, 16 * h : 16 * (h + 1)]), COPY)
 
-        gate = sb("gate", [P, PACK, J], F32)
-        for t in range(PACK):
-            qb = psum.tile([P, J], F32, name="q%d" % t)
-            nc.tensor.matmul_mx(out=qb[:], lhsT=ws_c[:, 256 * t : 256 * (t + 1)].bitcast(FP4X4), lhsT_scale=ws_s[:, P * t : P * (t + 1)],
-                                rhs=sx_c[:].bitcast(FP8X4), rhs_scale=sx_s[:], start=True, stop=True)
-            nc.scalar.activation(gate[:, t, :], qb[:], SIGMOID)
+        def product(bank, codes, scales, rhs, rhs_scale, u):
+            for e in range(2):
+                t = 2 * u + e
+                nc.tensor.matmul_mx(out=bank[:, e, :], lhsT=codes[:, 256 * t : 256 * (t + 1)].bitcast(FP4X4), lhsT_scale=scales[:, P * t : P * (t + 1)],
+                                    rhs=rhs.bitcast(FP8X4), rhs_scale=rhs_scale, start=True, stop=True)
+
+        def half(h):
+            return slice(HALF * h, HALF * (h + 1))
+
+        q_bank = {}
+        gate = {}
+
+        def logits(h, u):
+            q_bank[h, u] = psum.tile([P, 2, HALF], F32, name="q%d%d" % (h, u))
+            product(q_bank[h, u], ws_c, ws_s, sx_c[:, half(h)], sx_s[:, half(h)], u)
+
+        def sigmoid(h, u, dst):
+            gate[h, u] = dst
+            nc.scalar.activation(dst, q_bank[h, u][:], SIGMOID)
+
+        for h in range(2):
+            for u in range(2):
+                logits(h, u)
+        gate_first = sb("gate_first", [P, 2, HALF], F32)
+        sigmoid(0, 0, gate_first[:])
 
         gather(1, 0)
         gather(1, 1)
         w_c = deal_words("w_c", w_raw)
         gather(2, 0)
         gather(2, 1)
-        w_s = deal_scales("w_s", w_sraw, "x2")
 
-        xw = [sb("xw%d" % c, [P, CH, PACK], BF16) for c in range(NCH)]
-        xc = [sb("xc%d" % c, [P, CH], U32) for c in range(NCH)]
-        xs = [sb("xs%d" % c, [P, CH], U8) for c in range(NCH)]
+        xw = [sb("xw%d" % h, [P, HALF, PACK], BF16) for h in range(2)]
+        x_c = sb("x_c", [P, J], U32)
         y = [sb("y%d" % h, [P, PACK, HALF], F32) for h in range(2)]
-        yw = [sb("yw%d" % c, [P, CH, PACK], BF16) for c in range(NCH)]
+        yw = [sb("yw%d" % h, [P, HALF, PACK], BF16) for h in range(2)]
         y_c = sb("y_c", [P, J], U32)
         y_s = sb("y_s", [P, J], U8)
         ov = out_0.rearrange("(p t) j -> p t j", t=PACK)
         o1 = out_1[0].rearrange("p c r -> p (c r)").bitcast(I32)
-        pb = {}
+        p_bank = {}
 
-        def cols(c):
-            return slice(CH * (c % 2), CH * (c % 2 + 1))
+        def weave(copy, dst, src, a, b):
+            copy(out=dst[:, a:b, :].rearrange("p (g i) t -> p g t i", i=4), in_=src[:, :, a:b].rearrange("p t (g i) -> p g t i", i=4))
 
-        def weave(c, on_vector):
-            src = picked[c // 2][:, :, cols(c)].rearrange("p t j -> p j t")
-            if on_vector:
-                nc.vector.tensor_copy(out=xw[c][:], in_=src)
-            else:
-                nc.scalar.copy(out=xw[c][:], in_=src)
+        def quant(codes, scales, src, h):
+            nc.vector.quantize_mx(out=codes[:, half(h)].bitcast(FP8X4), scales=scales[:, half(h)], in_=src[:].rearrange("p j t -> p (j t)"))
 
-        def quant(c):
-            nc.vector.quantize_mx(out=xc[c][:].bitcast(FP8X4), scales=xs[c][:], in_=xw[c][:].rearrange("p j t -> p (j t)"))
-            pb[c] = psum.tile([P, PACK, CH], F32, name="p%d" % c)
-            for t in range(PACK):
-                nc.tensor.matmul_mx(out=pb[c][:, t, :], lhsT=w_c[:, 256 * t : 256 * (t + 1)].bitcast(FP4X4), lhsT_scale=w_s[:, P * t : P * (t + 1)],
-                                    rhs=xc[c][:].bitcast(FP8X4), rhs_scale=xs[c][:], start=True, stop=True)
+        def join(h):
+            for u in range(2):
+                p_bank[h, u] = psum.tile([P, 2, HALF], F32, name="p%d%d" % (h, u))
+                product(p_bank[h, u], w_c, w_s, x_c[:, half(h)], x_s[:, half(h)], u)
 
-        def gated(c):
-            nc.vector.tensor_tensor(y[c // 2][:, :, cols(c)], pb[c][:], gate[:, :, CH * c : CH * (c + 1)], MULT)
-
-        def store_y(h):
-            nc.sync.dma_start(out=ov[:, :, HALF * h : HALF * (h + 1)], in_=y[h][:])
-
-        def round_y(c, on_vector):
-            src = y[c // 2][:, :, cols(c)].rearrange("p t j -> p j t")
-            if on_vector:
-                nc.vector.tensor_copy(out=yw[c][:], in_=src)
-            else:
-                nc.scalar.copy(out=yw[c][:], in_=src)
-
-        def quant_y(c):
-            nc.vector.quantize_mx(out=y_c[:, CH * c : CH * (c + 1)].bitcast(FP8X4), scales=y_s[:, CH * c : CH * (c + 1)], in_=yw[c][:].rearrange("p j t -> p (j t)"))
+        def gated(h, u):
+            nc.vector.tensor_tensor(y[h][:, 2 * u : 2 * u + 2, :], p_bank[h, u][:], gate[h, u], MULT)
+            nc.sync.dma_start(out=ov[:, 2 * u : 2 * u + 2, half(h)], in_=y[h][:, 2 * u : 2 * u + 2, :])
 
         def store_words(h):
-            nc.sync.dma_start(out=o1[:, HALF * h : HALF * (h + 1)], in_=y_c[:, HALF * h : HALF * (h + 1)].bitcast(I32))
+            nc.sync.dma_start(out=o1[:, half(h)], in_=y_c[:, half(h)].bitcast(I32))
 
         gather(3, 0)
-        weave(0, True)
-        weave(1, False)
+        weave(nc.scalar.copy, xw[0], picked[0], 0, CH)
         gather(3, 1)
-        quant(0)
-        weave(2, False)
-        weave(3, False)
-        quant(1)
-        gated(0)
-        quant(2)
-        gated(1)
-        store_y(0)
-        round_y(0, False)
-        quant(3)
-        gated(2)
-        round_y(1, False)
-        gated(3)
-        store_y(1)
-        round_y(2, False)
-        quant_y(0)
-        quant_y(1)
+        weave(nc.vector.tensor_copy, xw[0], picked[0], CH, HALF)
+        weave(nc.scalar.copy, xw[1], picked[1], 0, HALF)
+        gate_rest = sb("gate_rest", [P, 3, 2, HALF], F32, "picked1")
+        sigmoid(0, 1, gate_rest[:, 0])
+        sigmoid(1, 0, gate_rest[:, 1])
+        sigmoid(1, 1, gate_rest[:, 2])
+        w_s = deal_scales("w_s", w_sraw)
+        x_s = sb("x_s", [P, J], U8, "w_sraw")
+        quant(x_c, x_s, xw[0], 0)
+        join(0)
+        quant(x_c, x_s, xw[1], 1)
+        join(1)
+        gated(0, 0)
+        gated(0, 1)
+        weave(nc.scalar.copy, yw[0], y[0], 0, HALF)
+        gated(1, 0)
+        gated(1, 1)
+        weave(nc.scalar.copy, yw[1], y[1], 0, CH)
+        weave(nc.vector.tensor_copy, yw[1], y[1], CH, HALF)
+        quant(y_c, y_s, yw[0], 0)
         store_words(0)
-        round_y(3, True)
-        quant_y(2)
-        quant_y(3)
+        quant(y_c, y_s, yw[1], 1)
         store_words(1)
         for q in range(4):
-            eng = nc.scalar if q % 2 else nc.sync
+            eng = nc.sync if q == 0 else nc.scalar
             eng.dma_start(out=out_2[0, 4 * q : 4 * q + 4, :].bitcast(I32), in_=y_s[32 * q : 32 * q + 4, :].bitcast(I32))

@@ -86,8 +86,8 @@ def tile_moe_expert_heads_gated_pl_kernel(tc, xt, w_words, w_scales, sx_words, s
 
         x0_bf = sb("x0_bf", [P, T], BF16)
         nc.scalar.activation(x0_bf[:], x[0][:], COPY)
-        for h in range(2):
-            nc.scalar.activation(picked[h][:, 0, :], x0_bf[:].indirect(offsets[:, 16 * h : 16 * (h + 1)]), COPY)
+        nc.scalar.activation(picked[0][:, 0, :], x0_bf[:].indirect(offsets[:, 0:16]), COPY)
+        gather(0, 1)
 
         def product(bank, codes, scales, rhs, rhs_scale, u):
             for e in range(2):
@@ -112,16 +112,21 @@ def tile_moe_expert_heads_gated_pl_kernel(tc, xt, w_words, w_scales, sx_words, s
         for h in range(2):
             for u in range(2):
                 logits(h, u)
-        gate_first = sb("gate_first", [P, 2, HALF], F32)
-        sigmoid(0, 0, gate_first[:])
+        xw = [sb("xw%d" % h, [P, HALF, PACK], BF16) for h in range(2)]
+
+        def weave_pair(h, u):
+            nc.scalar.copy(out=xw[h][:, :, 2 * u : 2 * u + 2], in_=picked[h][:, 2 * u : 2 * u + 2, :].rearrange("p t j -> p j t"))
 
         gather(1, 0)
         gather(1, 1)
+        weave_pair(0, 0)
+        weave_pair(1, 0)
+        gate_first = sb("gate_first", [P, 2, HALF], F32)
+        sigmoid(0, 0, gate_first[:])
         w_c = deal_words("w_c", w_raw)
         gather(2, 0)
         gather(2, 1)
 
-        xw = [sb("xw%d" % h, [P, HALF, PACK], BF16) for h in range(2)]
         x_c = sb("x_c", [P, J], U32)
         y = [sb("y%d" % h, [P, PACK, HALF], F32) for h in range(2)]
         yw = [sb("yw%d" % h, [P, HALF, PACK], BF16) for h in range(2)]
@@ -150,10 +155,9 @@ def tile_moe_expert_heads_gated_pl_kernel(tc, xt, w_words, w_scales, sx_words, s
             nc.sync.dma_start(out=o1[:, half(h)], in_=y_c[:, half(h)].bitcast(I32))
 
         gather(3, 0)
-        weave(nc.scalar.copy, xw[0], picked[0], 0, CH)
+        weave_pair(0, 1)
         gather(3, 1)
-        weave(nc.vector.tensor_copy, xw[0], picked[0], CH, HALF)
-        weave(nc.scalar.copy, xw[1], picked[1], 0, HALF)
+        weave_pair(1, 1)
         gate_rest = sb("gate_rest", [P, 3, 2, HALF], F32, "picked1")
         sigmoid(0, 1, gate_rest[:, 0])
         sigmoid(1, 0, gate_rest[:, 1])
@@ -169,8 +173,8 @@ def tile_moe_expert_heads_gated_pl_kernel(tc, xt, w_words, w_scales, sx_words, s
         weave(nc.scalar.copy, yw[0], y[0], 0, HALF)
         gated(1, 0)
         gated(1, 1)
-        weave(nc.scalar.copy, yw[1], y[1], 0, CH)
-        weave(nc.vector.tensor_copy, yw[1], y[1], CH, HALF)
+        weave(nc.scalar.copy, yw[1], y[1], 0, 160)
+        weave(nc.vector.tensor_copy, yw[1], y[1], 160, HALF)
         quant(y_c, y_s, yw[0], 0)
         store_words(0)
         quant(y_c, y_s, yw[1], 1)

@@ -19,9 +19,12 @@ MULT = mybir.AluOpType.mult
 
 P = 128
 PACK = 4
-HALF = 256
-CH = 128
-NCH = J // CH
+PAIR = 2
+HALF = J // 2
+LIST_COLS = HALF // 16
+QUADRANT = 32
+RUN = 4
+SCALAR_SLOTS = 80
 
 
 def tile_moe_expert_heads_gated_pl_kernel(tc, xt, w_words, w_scales, sx_words, sx_scales, ws_words, ws_scales, offs, out_0, out_1, out_2):
@@ -30,155 +33,153 @@ def tile_moe_expert_heads_gated_pl_kernel(tc, xt, w_words, w_scales, sx_words, s
         keep = ctx.enter_context(tc.tile_pool(name="keep", bufs=1))
         psum = ctx.enter_context(tc.psum_pool(name="psum", bufs=1))
 
-        def sb(name, shape, dtype, tag=None):
-            return keep.tile(shape, dtype, name=name, tag=tag or name, align_bytes=64)
-
-        offsets = keep.tile([P, J // 16], U16, name="offsets")
-        w_raw = sb("w_raw", [P, 2 * N], U8)
-        ws_raw = sb("ws_raw", [P, 2 * N], U8)
-        w_sraw = sb("w_sraw", [P, N], U8)
-        ws_sraw = sb("ws_sraw", [P, N], U8)
-        sx_c = sb("sx_c", [P, J], U32)
-        sx_s = sb("sx_s", [P, J], U8)
-        x = [sb("x%d" % t, [P, T], F32) for t in range(PACK)]
-        warm = sb("warm", [P, 1], F32)
-        warm2 = sb("warm2", [P, 1], F32)
-
-        def load_scales(eng, tile, src):
-            for q in range(4):
-                eng.dma_start(out=tile[32 * q : 32 * q + 4, :].bitcast(I32), in_=src[0, 4 * q : 4 * q + 4, :].bitcast(I32))
-
-        xv = xt.rearrange("(p t) c -> p t c", t=PACK)
-        nc.vector.memset(warm[:], 0.0)
-        nc.vector.memset(ws_sraw[:].bitcast(I32), 0)
-        nc.vector.memset(sx_s[:].bitcast(I32), 0)
-        nc.vector.memset(w_sraw[:].bitcast(I32), 0)
-        nc.scalar.activation(warm2[:], warm[:], SIGMOID)
-        nc.sync.dma_start(offsets[:], offs)
-        nc.sync.dma_start(out=ws_raw[:].bitcast(I32), in_=ws_words[0].bitcast(I32))
-        nc.sync.dma_start(out=x[0][:], in_=xv[:, 0, :])
-        load_scales(nc.sync, ws_sraw, ws_scales)
-        nc.sync.dma_start(out=x[1][:], in_=xv[:, 1, :])
-        nc.sync.dma_start(out=w_raw[:].bitcast(I32), in_=w_words[0].bitcast(I32))
-        nc.sync.dma_start(out=x[2][:], in_=xv[:, 2, :])
-        nc.sync.dma_start(out=sx_c[:].bitcast(I32), in_=sx_words[0].rearrange("p c r -> p (c r)").bitcast(I32))
-        load_scales(nc.sync, sx_s, sx_scales)
-        nc.sync.dma_start(out=x[3][:], in_=xv[:, 3, :])
-        load_scales(nc.sync, w_sraw, w_scales)
-
-        def deal_words(name, raw):
-            dealt = sb(name, [P, 2 * N], U8)
-            nc.vector.tensor_copy(out=dealt[:].bitcast(U16).rearrange("p (t m) -> p t m", t=PACK), in_=raw[:].bitcast(U16).rearrange("p (m t) -> p t m", t=PACK))
-            return dealt
-
-        def deal_scales(name, raw, tag=None):
-            dealt = sb(name, [P, N], U8, tag)
-            nc.vector.tensor_copy(out=dealt[:].rearrange("p (t m) -> p t m", t=PACK), in_=raw[:].rearrange("p (m t) -> p t m", t=PACK))
-            return dealt
-
-        ws_c = deal_words("ws_c", ws_raw)
-        ws_s = deal_scales("ws_s", ws_sraw)
-
-        picked = [sb("picked%d" % h, [P, PACK, HALF], BF16) for h in range(2)]
-
-        def gather(t, h):
-            nc.vector.tensor_copy(picked[h][:, t, :], x[t][:].indirect(offsets[:, 16 * h : 16 * (h + 1)]))
-
-        x0_bf = sb("x0_bf", [P, T], BF16)
-        nc.scalar.activation(x0_bf[:], x[0][:], COPY)
-        nc.scalar.activation(picked[0][:, 0, :], x0_bf[:].indirect(offsets[:, 0:16]), COPY)
-        gather(0, 1)
-
-        def product(bank, codes, scales, rhs, rhs_scale, u):
-            for e in range(2):
-                t = 2 * u + e
-                nc.tensor.matmul_mx(out=bank[:, e, :], lhsT=codes[:, 256 * t : 256 * (t + 1)].bitcast(FP4X4), lhsT_scale=scales[:, P * t : P * (t + 1)],
-                                    rhs=rhs.bitcast(FP8X4), rhs_scale=rhs_scale, start=True, stop=True)
+        def sbuf(name, shape, dtype, in_place_of=None):
+            return keep.tile(shape, dtype, name=name, tag=in_place_of or name, align_bytes=64)
 
         def half(h):
             return slice(HALF * h, HALF * (h + 1))
 
-        q_bank = {}
+        def pair(u):
+            return slice(PAIR * u, PAIR * (u + 1))
+
+        offsets = keep.tile([P, J // 16], U16, name="offsets")
+        w_raw = sbuf("w_raw", [P, 2 * N], U8)
+        ws_raw = sbuf("ws_raw", [P, 2 * N], U8)
+        w_scale_raw = sbuf("w_scale_raw", [P, N], U8)
+        ws_scale_raw = sbuf("ws_scale_raw", [P, N], U8)
+        sx_codes = sbuf("sx_codes", [P, J], U32)
+        sx_scale = sbuf("sx_scale", [P, J], U8)
+        x = [sbuf("x%d" % t, [P, T], F32) for t in range(PACK)]
+        warm_in = sbuf("warm_in", [P, 1], F32)
+        warm_out = sbuf("warm_out", [P, 1], F32)
+
+        def load_scales(tile, src):
+            for quad in range(4):
+                nc.sync.dma_start(out=tile[QUADRANT * quad : QUADRANT * quad + 4, :].bitcast(I32), in_=src[0, 4 * quad : 4 * quad + 4, :].bitcast(I32))
+
+        x_planes = xt.rearrange("(p t) c -> p t c", t=PACK)
+        nc.vector.memset(warm_in[:], 0.0)
+        nc.vector.memset(ws_scale_raw[:].bitcast(I32), 0)
+        nc.vector.memset(sx_scale[:].bitcast(I32), 0)
+        nc.vector.memset(w_scale_raw[:].bitcast(I32), 0)
+        nc.scalar.activation(warm_out[:], warm_in[:], SIGMOID)
+        nc.sync.dma_start(offsets[:], offs)
+        nc.sync.dma_start(out=ws_raw[:].bitcast(I32), in_=ws_words[0].bitcast(I32))
+        nc.sync.dma_start(out=x[0][:], in_=x_planes[:, 0, :])
+        load_scales(ws_scale_raw, ws_scales)
+        nc.sync.dma_start(out=x[1][:], in_=x_planes[:, 1, :])
+        nc.sync.dma_start(out=w_raw[:].bitcast(I32), in_=w_words[0].bitcast(I32))
+        nc.sync.dma_start(out=x[2][:], in_=x_planes[:, 2, :])
+        nc.sync.dma_start(out=sx_codes[:].bitcast(I32), in_=sx_words[0].rearrange("p c r -> p (c r)").bitcast(I32))
+        load_scales(sx_scale, sx_scales)
+        nc.sync.dma_start(out=x[3][:], in_=x_planes[:, 3, :])
+        load_scales(w_scale_raw, w_scales)
+
+        def deal_words(name, raw):
+            dealt = sbuf(name, [P, 2 * N], U8)
+            nc.vector.tensor_copy(out=dealt[:].bitcast(U16).rearrange("p (t m) -> p t m", t=PACK), in_=raw[:].bitcast(U16).rearrange("p (m t) -> p t m", t=PACK))
+            return dealt
+
+        def deal_scales(name, raw):
+            dealt = sbuf(name, [P, N], U8)
+            nc.vector.tensor_copy(out=dealt[:].rearrange("p (t m) -> p t m", t=PACK), in_=raw[:].rearrange("p (m t) -> p t m", t=PACK))
+            return dealt
+
+        ws_codes = deal_words("ws_codes", ws_raw)
+        ws_scale = deal_scales("ws_scale", ws_scale_raw)
+
+        picked = [sbuf("picked%d" % h, [P, PACK, HALF], BF16) for h in range(2)]
+
+        def entries(h):
+            return offsets[:, LIST_COLS * h : LIST_COLS * (h + 1)]
+
+        def gather(t, h):
+            nc.vector.tensor_copy(picked[h][:, t, :], x[t][:].indirect(entries(h)))
+
+        x0_rounded = sbuf("x0_rounded", [P, T], BF16)
+        nc.scalar.activation(x0_rounded[:], x[0][:], COPY)
+        nc.scalar.activation(picked[0][:, 0, :], x0_rounded[:].indirect(entries(0)), COPY)
+        gather(0, 1)
+
+        def product(name, codes, scale, moving, moving_scale, h, u):
+            bank = psum.tile([P, PAIR, HALF], F32, name="%s%d%d" % (name, h, u))
+            for e in range(PAIR):
+                t = PAIR * u + e
+                nc.tensor.matmul_mx(out=bank[:, e, :], lhsT=codes[:, 2 * P * t : 2 * P * (t + 1)].bitcast(FP4X4), lhsT_scale=scale[:, P * t : P * (t + 1)],
+                                    rhs=moving[:, half(h)].bitcast(FP8X4), rhs_scale=moving_scale[:, half(h)], start=True, stop=True)
+            return bank
+
+        pieces = [(h, u) for h in range(2) for u in range(2)]
+        q_bank = {(h, u): product("q", ws_codes, ws_scale, sx_codes, sx_scale, h, u) for h, u in pieces}
         gate = {}
 
-        def logits(h, u):
-            q_bank[h, u] = psum.tile([P, 2, HALF], F32, name="q%d%d" % (h, u))
-            product(q_bank[h, u], ws_c, ws_s, sx_c[:, half(h)], sx_s[:, half(h)], u)
+        def sigmoid(piece, dst):
+            gate[piece] = dst
+            nc.scalar.activation(dst, q_bank[piece][:], SIGMOID)
 
-        def sigmoid(h, u, dst):
-            gate[h, u] = dst
-            nc.scalar.activation(dst, q_bank[h, u][:], SIGMOID)
-
-        for h in range(2):
-            for u in range(2):
-                logits(h, u)
-        xw = [sb("xw%d" % h, [P, HALF, PACK], BF16) for h in range(2)]
+        x_woven = [sbuf("x_woven%d" % h, [P, HALF, PACK], BF16) for h in range(2)]
 
         def weave_pair(h, u):
-            nc.scalar.copy(out=xw[h][:, :, 2 * u : 2 * u + 2], in_=picked[h][:, 2 * u : 2 * u + 2, :].rearrange("p t j -> p j t"))
+            nc.scalar.copy(out=x_woven[h][:, :, pair(u)], in_=picked[h][:, pair(u), :].rearrange("p t j -> p j t"))
 
         gather(1, 0)
         gather(1, 1)
         weave_pair(0, 0)
         weave_pair(1, 0)
-        gate_first = sb("gate_first", [P, 2, HALF], F32)
-        sigmoid(0, 0, gate_first[:])
-        w_c = deal_words("w_c", w_raw)
+        gate_first = sbuf("gate_first", [P, PAIR, HALF], F32)
+        sigmoid(pieces[0], gate_first[:])
+        w_codes = deal_words("w_codes", w_raw)
         gather(2, 0)
         gather(2, 1)
 
-        x_c = sb("x_c", [P, J], U32)
-        y = [sb("y%d" % h, [P, PACK, HALF], F32) for h in range(2)]
-        yw = [sb("yw%d" % h, [P, HALF, PACK], BF16) for h in range(2)]
-        y_c = sb("y_c", [P, J], U32)
-        y_s = sb("y_s", [P, J], U8)
-        ov = out_0.rearrange("(p t) j -> p t j", t=PACK)
-        o1 = out_1[0].rearrange("p c r -> p (c r)").bitcast(I32)
+        x_codes = sbuf("x_codes", [P, J], U32)
+        y = [sbuf("y%d" % h, [P, PACK, HALF], F32) for h in range(2)]
+        y_woven = [sbuf("y_woven%d" % h, [P, HALF, PACK], BF16) for h in range(2)]
+        y_codes = sbuf("y_codes", [P, J], U32)
+        y_scale = sbuf("y_scale", [P, J], U8)
+        out_planes = out_0.rearrange("(p t) j -> p t j", t=PACK)
+        out_words = out_1[0].rearrange("p c r -> p (c r)").bitcast(I32)
         p_bank = {}
 
-        def weave(copy, dst, src, a, b):
-            copy(out=dst[:, a:b, :].rearrange("p (g i) t -> p g t i", i=4), in_=src[:, :, a:b].rearrange("p t (g i) -> p g t i", i=4))
+        def quantise(codes, scale, woven, h):
+            nc.vector.quantize_mx(out=codes[:, half(h)].bitcast(FP8X4), scales=scale[:, half(h)], in_=woven[h][:].rearrange("p j t -> p (j t)"))
 
-        def quant(codes, scales, src, h):
-            nc.vector.quantize_mx(out=codes[:, half(h)].bitcast(FP8X4), scales=scales[:, half(h)], in_=src[:].rearrange("p j t -> p (j t)"))
-
-        def join(h):
+        def join_groups(h):
             for u in range(2):
-                p_bank[h, u] = psum.tile([P, 2, HALF], F32, name="p%d%d" % (h, u))
-                product(p_bank[h, u], w_c, w_s, x_c[:, half(h)], x_s[:, half(h)], u)
+                p_bank[h, u] = product("p", w_codes, w_scale, x_codes, x_scale, h, u)
 
-        def gated(h, u):
-            nc.vector.tensor_tensor(y[h][:, 2 * u : 2 * u + 2, :], p_bank[h, u][:], gate[h, u], MULT)
-            nc.sync.dma_start(out=ov[:, 2 * u : 2 * u + 2, half(h)], in_=y[h][:, 2 * u : 2 * u + 2, :])
+        def gate_and_store(h, u):
+            nc.vector.tensor_tensor(y[h][:, pair(u), :], p_bank[h, u][:], gate[h, u], MULT)
+            nc.sync.dma_start(out=out_planes[:, pair(u), half(h)], in_=y[h][:, pair(u), :])
+
+        def round_y(copy, h, first, end):
+            copy(out=y_woven[h][:, first:end, :].rearrange("p (g i) t -> p g t i", i=RUN), in_=y[h][:, :, first:end].rearrange("p t (g i) -> p g t i", i=RUN))
 
         def store_words(h):
-            nc.sync.dma_start(out=o1[:, half(h)], in_=y_c[:, half(h)].bitcast(I32))
+            nc.sync.dma_start(out=out_words[:, half(h)], in_=y_codes[:, half(h)].bitcast(I32))
 
         gather(3, 0)
         weave_pair(0, 1)
         gather(3, 1)
         weave_pair(1, 1)
-        gate_rest = sb("gate_rest", [P, 3, 2, HALF], F32, "picked1")
-        sigmoid(0, 1, gate_rest[:, 0])
-        sigmoid(1, 0, gate_rest[:, 1])
-        sigmoid(1, 1, gate_rest[:, 2])
-        w_s = deal_scales("w_s", w_sraw)
-        x_s = sb("x_s", [P, J], U8, "w_sraw")
-        quant(x_c, x_s, xw[0], 0)
-        join(0)
-        quant(x_c, x_s, xw[1], 1)
-        join(1)
-        gated(0, 0)
-        gated(0, 1)
-        weave(nc.scalar.copy, yw[0], y[0], 0, HALF)
-        gated(1, 0)
-        gated(1, 1)
-        weave(nc.scalar.copy, yw[1], y[1], 0, 160)
-        weave(nc.vector.tensor_copy, yw[1], y[1], 160, HALF)
-        quant(y_c, y_s, yw[0], 0)
-        store_words(0)
-        quant(y_c, y_s, yw[1], 1)
-        store_words(1)
-        for q in range(4):
-            eng = nc.sync if q == 0 else nc.scalar
-            eng.dma_start(out=out_2[0, 4 * q : 4 * q + 4, :].bitcast(I32), in_=y_s[32 * q : 32 * q + 4, :].bitcast(I32))
+        gate_rest = sbuf("gate_rest", [P, len(pieces) - 1, PAIR, HALF], F32, "picked1")
+        for i, piece in enumerate(pieces[1:]):
+            sigmoid(piece, gate_rest[:, i])
+        w_scale = deal_scales("w_scale", w_scale_raw)
+        x_scale = sbuf("x_scale", [P, J], U8, "w_scale_raw")
+        for h in range(2):
+            quantise(x_codes, x_scale, x_woven, h)
+            join_groups(h)
+        gate_and_store(0, 0)
+        gate_and_store(0, 1)
+        round_y(nc.scalar.copy, 0, 0, HALF)
+        gate_and_store(1, 0)
+        gate_and_store(1, 1)
+        round_y(nc.scalar.copy, 1, 0, SCALAR_SLOTS)
+        round_y(nc.vector.tensor_copy, 1, SCALAR_SLOTS, HALF)
+        for h in range(2):
+            quantise(y_codes, y_scale, y_woven, h)
+            store_words(h)
+        for quad in range(4):
+            queue = nc.sync if quad == 0 else nc.scalar
+            queue.dma_start(out=out_2[0, 4 * quad : 4 * quad + 4, :].bitcast(I32), in_=y_scale[QUADRANT * quad : QUADRANT * quad + 4, :].bitcast(I32))

from contextlib import ExitStack

import concourse.mybir as mybir

K, T, J, L, N = 512, 1024, 512, 512, 512
FLOPS = 2 * K * N * J + 2 * L * N * J

F32 = mybir.dt.float32
BF16 = mybir.dt.bfloat16
I32 = mybir.dt.int32
U32 = mybir.dt.uint32
U16 = mybir.dt.uint16
U8 = mybir.dt.uint8
FP8X4 = mybir.dt.float8_e4m3fn_x4
FP4X4 = mybir.dt.float4_e2m1fn_x4
SIGMOID = mybir.ActivationFunctionType.Sigmoid
COPY = mybir.ActivationFunctionType.Copy
MULT = mybir.AluOpType.mult

P = 128
PACK = 4
PAIR = 2
HALF = J // 2
LIST_COLS = HALF // 16
QUADRANT = 32
RUN = 4
SCALAR_SLOTS = 80


def tile_moe_expert_heads_gated_pl_kernel(tc, xt, w_words, w_scales, sx_words, sx_scales, ws_words, ws_scales, offs, out_0, out_1, out_2):
    nc = tc.nc
    with ExitStack() as ctx:
        keep = ctx.enter_context(tc.tile_pool(name="keep", bufs=1))
        psum = ctx.enter_context(tc.psum_pool(name="psum", bufs=1))

        def sbuf(name, shape, dtype, in_place_of=None):
            return keep.tile(shape, dtype, name=name, tag=in_place_of or name, align_bytes=64)

        def half(h):
            return slice(HALF * h, HALF * (h + 1))

        def pair(u):
            return slice(PAIR * u, PAIR * (u + 1))

        offsets = keep.tile([P, J // 16], U16, name="offsets")
        w_raw = sbuf("w_raw", [P, 2 * N], U8)
        ws_raw = sbuf("ws_raw", [P, 2 * N], U8)
        w_scale_raw = sbuf("w_scale_raw", [P, N], U8)
        ws_scale_raw = sbuf("ws_scale_raw", [P, N], U8)
        sx_codes = sbuf("sx_codes", [P, J], U32)
        sx_scale = sbuf("sx_scale", [P, J], U8)
        x = [sbuf("x%d" % t, [P, T], F32) for t in range(PACK)]
        warm_in = sbuf("warm_in", [P, 1], F32)
        warm_out = sbuf("warm_out", [P, 1], F32)

        def load_scales(tile, src):
            for quad in range(4):
                nc.sync.dma_start(out=tile[QUADRANT * quad : QUADRANT * quad + 4, :].bitcast(I32), in_=src[0, 4 * quad : 4 * quad + 4, :].bitcast(I32))

        x_planes = xt.rearrange("(p t) c -> p t c", t=PACK)
        nc.vector.memset(warm_in[:], 0.0)
        nc.vector.memset(ws_scale_raw[:].bitcast(I32), 0)
        nc.vector.memset(sx_scale[:].bitcast(I32), 0)
        nc.vector.memset(w_scale_raw[:].bitcast(I32), 0)
        nc.scalar.activation(warm_out[:], warm_in[:], SIGMOID)
        nc.sync.dma_start(offsets[:], offs)
        nc.sync.dma_start(out=ws_raw[:].bitcast(I32), in_=ws_words[0].bitcast(I32))
        nc.sync.dma_start(out=x[0][:], in_=x_planes[:, 0, :])
        load_scales(ws_scale_raw, ws_scales)
        nc.sync.dma_start(out=x[1][:], in_=x_planes[:, 1, :])
        nc.sync.dma_start(out=w_raw[:].bitcast(I32), in_=w_words[0].bitcast(I32))
        nc.sync.dma_start(out=x[2][:], in_=x_planes[:, 2, :])
        nc.sync.dma_start(out=sx_codes[:].bitcast(I32), in_=sx_words[0].rearrange("p c r -> p (c r)").bitcast(I32))
        load_scales(sx_scale, sx_scales)
        nc.sync.dma_start(out=x[3][:], in_=x_planes[:, 3, :])
        load_scales(w_scale_raw, w_scales)

        def deal_words(name, raw):
            dealt = sbuf(name, [P, 2 * N], U8)
            nc.vector.tensor_copy(out=dealt[:].bitcast(U16).rearrange("p (t m) -> p t m", t=PACK), in_=raw[:].bitcast(U16).rearrange("p (m t) -> p t m", t=PACK))
            return dealt

        def deal_scales(name, raw):
            dealt = sbuf(name, [P, N], U8)
            nc.vector.tensor_copy(out=dealt[:].rearrange("p (t m) -> p t m", t=PACK), in_=raw[:].rearrange("p (m t) -> p t m", t=PACK))
            return dealt

        ws_codes = deal_words("ws_codes", ws_raw)
        ws_scale = deal_scales("ws_scale", ws_scale_raw)

        picked = [sbuf("picked%d" % h, [P, PACK, HALF], BF16) for h in range(2)]

        def entries(h):
            return offsets[:, LIST_COLS * h : LIST_COLS * (h + 1)]

        def gather(t, h):
            nc.vector.tensor_copy(picked[h][:, t, :], x[t][:].indirect(entries(h)))

        x0_rounded = sbuf("x0_rounded", [P, T], BF16)
        nc.scalar.activation(x0_rounded[:], x[0][:], COPY)
        nc.scalar.activation(picked[0][:, 0, :], x0_rounded[:].indirect(entries(0)), COPY)
        gather(0, 1)

        def product(name, codes, scale, moving, moving_scale, h, u):
            bank = psum.tile([P, PAIR, HALF], F32, name="%s%d%d" % (name, h, u))
            for e in range(PAIR):
                t = PAIR * u + e
                nc.tensor.matmul_mx(out=bank[:, e, :], lhsT=codes[:, 2 * P * t : 2 * P * (t + 1)].bitcast(FP4X4), lhsT_scale=scale[:, P * t : P * (t + 1)],
                                    rhs=moving[:, half(h)].bitcast(FP8X4), rhs_scale=moving_scale[:, half(h)], start=True, stop=True)
            return bank

        pieces = [(h, u) for h in range(2) for u in range(2)]
        q_bank = {(h, u): product("q", ws_codes, ws_scale, sx_codes, sx_scale, h, u) for h, u in pieces}
        gate = {}

        def sigmoid(piece, dst):
            gate[piece] = dst
            nc.scalar.activation(dst, q_bank[piece][:], SIGMOID)

        x_woven = [sbuf("x_woven%d" % h, [P, HALF, PACK], BF16) for h in range(2)]

        def weave_pair(h, u):
            nc.scalar.copy(out=x_woven[h][:, :, pair(u)], in_=picked[h][:, pair(u), :].rearrange("p t j -> p j t"))

        gather(1, 0)
        gather(1, 1)
        weave_pair(0, 0)
        weave_pair(1, 0)
        gate_first = sbuf("gate_first", [P, PAIR, HALF], F32)
        sigmoid(pieces[0], gate_first[:])
        w_codes = deal_words("w_codes", w_raw)
        gather(2, 0)
        gather(2, 1)

        x_codes = sbuf("x_codes", [P, J], U32)
        y = [sbuf("y%d" % h, [P, PACK, HALF], F32) for h in range(2)]
        y_woven = [sbuf("y_woven%d" % h, [P, HALF, PACK], BF16) for h in range(2)]
        y_codes = sbuf("y_codes", [P, J], U32)
        y_scale = sbuf("y_scale", [P, J], U8)
        out_planes = out_0.rearrange("(p t) j -> p t j", t=PACK)
        out_words = out_1[0].rearrange("p c r -> p (c r)").bitcast(I32)
        p_bank = {}

        def quantise(codes, scale, woven, h):
            nc.vector.quantize_mx(out=codes[:, half(h)].bitcast(FP8X4), scales=scale[:, half(h)], in_=woven[h][:].rearrange("p j t -> p (j t)"))

        def join_groups(h):
            for u in range(2):
                p_bank[h, u] = product("p", w_codes, w_scale, x_codes, x_scale, h, u)

        def gate_and_store(h, u):
            nc.vector.tensor_tensor(y[h][:, pair(u), :], p_bank[h, u][:], gate[h, u], MULT)
            nc.sync.dma_start(out=out_planes[:, pair(u), half(h)], in_=y[h][:, pair(u), :])

        def round_y(copy, h, first, end):
            copy(out=y_woven[h][:, first:end, :].rearrange("p (g i) t -> p g t i", i=RUN), in_=y[h][:, :, first:end].rearrange("p t (g i) -> p g t i", i=RUN))

        def store_words(h):
            nc.sync.dma_start(out=out_words[:, half(h)], in_=y_codes[:, half(h)].bitcast(I32))

        gather(3, 0)
        weave_pair(0, 1)
        gather(3, 1)
        weave_pair(1, 1)
        gate_rest = sbuf("gate_rest", [P, len(pieces) - 1, PAIR, HALF], F32, "picked1")
        for i, piece in enumerate(pieces[1:]):
            sigmoid(piece, gate_rest[:, i])
        w_scale = deal_scales("w_scale", w_scale_raw)
        x_scale = sbuf("x_scale", [P, J], U8, "w_scale_raw")
        for h in range(2):
            quantise(x_codes, x_scale, x_woven, h)
            join_groups(h)
        gate_and_store(0, 0)
        gate_and_store(0, 1)
        round_y(nc.scalar.copy, 0, 0, HALF)
        gate_and_store(1, 0)
        gate_and_store(1, 1)
        round_y(nc.scalar.copy, 1, 0, SCALAR_SLOTS)
        round_y(nc.vector.tensor_copy, 1, SCALAR_SLOTS, HALF)
        for h in range(2):
            quantise(y_codes, y_scale, y_woven, h)
            store_words(h)
        for quad in range(4):
            queue = nc.sync if quad == 0 else nc.scalar
            queue.dma_start(out=out_2[0, 4 * quad : 4 * quad + 4, :].bitcast(I32), in_=y_scale[QUADRANT * quad : QUADRANT * quad + 4, :].bitcast(I32))
